import numpy as np, ml_dtypes
CORES = [8,136,40,168]
N = 4
BF = ml_dtypes.bfloat16
R, D, CAP, MEETS = 8, 4, 96, (1, 2)
L = R * 4 ** D; P = (4 * L - R) // 3; I = P - L
OFF = [(R * 4 ** t - R) // 3 for t in range(D + 2)]
NODE = np.arange(P)
def rebuild(v):
    for t in range(D - 1, -1, -1):
        k = v[..., OFF[t + 1]:OFF[t + 2]]
        v[..., OFF[t]:OFF[t + 1]] = (k[..., 0::4] + 3 * k[..., 1::4] + 5 * k[..., 2::4] + 7 * k[..., 3::4]) & 255
    return v
def places(kids):
    c = kids.reshape(N, 8, 4, P); pl = np.zeros((N, 8, P), np.int64); pl[..., :R] = np.arange(R)
    for t in range(D):
        k = np.take_along_axis(c, pl[:, :, None, OFF[t]:OFF[t + 1]], 3)
        pl[..., OFF[t + 1]:OFF[t + 2]] = k.transpose(0, 1, 3, 2).reshape(N, 8, -1)
    return pl
def logical(dg, pl):
    return np.take_along_axis(dg.astype(np.float32).astype(np.int32).reshape(N, 8, 16, P), pl[:, :, None], 3)
def opened(v, m):
    o = np.any(v != v[np.arange(N) ^ m], axis=2)
    for t in range(D):
        o[..., OFF[t + 1]:OFF[t + 2]] &= np.repeat(o[..., OFF[t]:OFF[t + 1]], 4, axis=-1)
    return o
def meet(v, m):
    o = opened(v, m); u = v[np.arange(N) ^ m]; w = v.copy()
    up = o[..., I:] & (u[:, :, 15, I:] > v[:, :, 15, I:])
    w[..., I:] = np.where(up[:, :, None], u[..., I:], v[..., I:])
    return rebuild(w)
def put(rng, v):
    pl = np.concatenate([np.broadcast_to(np.arange(R), (N, 8, R)), R + np.argsort(rng.random((N, 8, P - R)), axis=-1)], axis=-1)
    k = np.zeros((N, 8, 4, P), np.int32); np.put_along_axis(k, pl[:, :, None, :I], pl[..., R:].reshape(N, 8, I, 4).transpose(0, 1, 3, 2).astype(np.int32), 3)
    e = np.zeros((N, 8, 16, P), np.float32); np.put_along_axis(e, pl[:, :, None], v.astype(np.float32), 3)
    return {"dg": e.reshape(N, 128, P).astype(BF), "kids": k.reshape(N, 32, P)}
def whole(rng, *shape):
    return rng.integers(0, 256, shape, dtype=np.int32)
def pool(rng):
    par = np.argsort(rng.random((8, L // 4)), axis=1)[:, :CAP // 8]; m = np.zeros((8, L // 4, 4), bool); np.put_along_axis(m, par[:, :, None], True, 1)
    m = m.reshape(8, L); np.put_along_axis(m, np.argsort(rng.random((8, L)), axis=1)[:, :CAP // 2 - 2], True, 1); m[:, 0] = True; m[:, -1] = True
    return m, par
def change(rng, base, m, x):
    mod = m & (rng.random((N, 8, L)) < 0.6); one = rng.random((N, 8, 1, L)) < 0.3
    c = mod[:, :, None] & (~one | (np.arange(16)[:, None] == rng.integers(0, 16, (N, 8, 1, L))))
    c[:, :, 15] &= rng.random((N, 8, L)) >= 0.25
    return np.ascontiguousarray(np.where(c, x, base))
def collide(rng, base, x, par):
    k = np.take_along_axis(base.reshape(8, 16, L // 4, 4), par[:, None, :, None], 2); k = np.repeat(k[None], N, axis=0)
    e = rng.integers(1, 256, k.shape[:-1], dtype=np.int32); k[..., 0] = (k[..., 0] - 3 * e) & 255; k[..., 1] = (k[..., 1] + e) & 255
    w = x.reshape(N, 8, 16, L // 4, 4).copy(); np.put_along_axis(w, par[None, :, None, :, None], k, 3); return w.reshape(N, 8, 16, L)
def grow(rng, base, x, m, hide, own):
    v = np.zeros((N, 8, 16, P), np.int32); v[..., I:] = x; rebuild(v); b = np.zeros((8, 16, P), np.int32); b[..., I:] = base; rebuild(b)
    cl = np.zeros((8, P), bool); cl[:, I:] = m
    for t in range(D - 1, -1, -1):
        cl[:, OFF[t]:OFF[t + 1]] = np.any(cl[:, OFF[t + 1]:OFF[t + 2]].reshape(8, -1, 4), axis=2)
    h = cl & (rng.random((8, P)) < hide) & (NODE < I); v = np.where(h[:, None], b, v)
    o = cl & (rng.random((N, 8, P)) < own) & (NODE < I); v = np.where(o[:, :, None], whole(rng, N, 8, 16, P), v)
    s = ~cl & (rng.random((8, P)) < 0.02) & (NODE < I)
    return np.where(s[:, None], whole(rng, 8, 16, P), v)
def balance(rng, v, m):
    a = np.arange(16)[:, None]; low = (np.arange(N) < (np.arange(N) ^ MEETS[0]))[:, None, None, None]
    for t in range(D):
        n = R * 4 ** t; k = np.any(m.reshape(8, n, -1), axis=2)
        e = rng.integers(1, 32, (N, 8, 1, n)) * rng.choice(np.array([-1, 1]), (N, 8, 1, n))
        if t % 2 == 0:
            s = rng.integers(0, 16, (N, 8, 1, n)); c = 1 * (a == s) - 1 * (a == ((s + rng.integers(1, 16, (N, 8, 1, n))) & 15))
        else:
            s = rng.integers(0, 14, (N, 8, 1, n)); c = 1 * (a == s) - 2 * (a == s + 1) + 1 * (a == s + 2)
        z = rng.integers(64, 192, (8, 16, n)) + low * e * c
        v[..., OFF[t]:OFF[t + 1]] = np.where(k[:, None], z, v[..., OFF[t]:OFF[t + 1]])
    return v
def setup_inputs(rng):
    base = whole(rng, 8, 16, L); m, par = pool(rng); x = change(rng, base, m, whole(rng, N, 8, 16, L)); x = collide(rng, base, x, par[:, :CAP // 32])
    return put(rng, grow(rng, base, x, m, 0.1 * (NODE >= OFF[D - 1]), 0.05))
def setup_inputs_full(rng):
    base = whole(rng, 8, 16, L); m = np.zeros((8, L), bool); t = [t for t in range(D + 1) if R * 4 ** t >= CAP][0]; w = 4 ** (D - t)
    for i, g in enumerate(rng.permutation(8)):
        if i % 4 == 1: l = (4 * rng.permutation(L // 4)[:CAP // 4, None] + np.arange(4)).reshape(-1)
        elif i % 4 == 3: l = np.arange(L - CAP, L)
        else: l = rng.permutation(R * 4 ** t)[:CAP] * w + rng.integers(0, w, CAP)
        m[g, l] = True
    z = whole(rng, N, 8, 16, L)
    for s in (0, 15): z[:, :, s] = (z[0, :, s].copy() + 31 * np.arange(N)[:, None, None]) & 255
    v = grow(rng, base, np.where(m[:, None], z, base), m, 0.0, 0.0)
    return put(rng, balance(rng, v, m & (rng.random((8, L)) < 0.5)))
def setup_inputs_ties(rng):
    base = whole(rng, 8, 16, L); base[:, 15] = rng.choice(np.array([0, 1, 254, 255]), (8, L)); m, par = pool(rng)
    x = change(rng, base, m, whole(rng, N, 8, 16, L)); c = np.any(x != base, axis=2)
    x[:, :, 15] = np.where(c, np.clip(base[:, 15] + rng.choice(np.array([-1, 0, 0, 1]), (N, 8, L)), 0, 255), base[:, 15])
    return put(rng, grow(rng, base, x, m, 0.0, 0.05))
def setup_inputs_hidden(rng):
    base = whole(rng, 8, 16, L); m, par = pool(rng); x = change(rng, base, m, whole(rng, N, 8, 16, L)); x = collide(rng, base, x, par)
    return put(rng, grow(rng, base, x, m, 0.15, 0.3))
def setup_inputs_calm(rng):
    base = whole(rng, 8, 16, L); m, par = pool(rng); p = rng.permutation(8); a = int(rng.integers(0, N)); m[p[:5]] = False; m[p[3], 0] = True; m[p[4], -1] = True
    x = change(rng, base, m, whole(rng, N, 8, 16, L))
    for g, l in ((p[3], 0), (p[4], L - 1)):
        x[:, g, :, l] = base[g, :, l]; x[a ^ MEETS[1], g, :, l] = (base[g, :, l] + rng.integers(1, 256, 16)) & 255
    v = grow(rng, base, x, m, 0.0, 0.0); v[a ^ MEETS[0]] = v[a]; return put(rng, v)
def setup_inputs_spread(rng):
    def uneven(*shape):
        u = rng.random(shape, dtype=np.float32); u = u * u * u; u = np.minimum(256 * u * u, 255).astype(np.int32)
        return np.where(rng.random(shape, dtype=np.float32) < 0.1, np.int32(255), u)
    base = uneven(8, 16, L) * (rng.random((8, 1, L)) > 0.0625).astype(np.int32); m, par = pool(rng)
    x = change(rng, base, m, uneven(N, 8, 16, L)); x = collide(rng, base, x, par[:, :CAP // 32])
    return put(rng, grow(rng, base, x, m, 0.1 * (NODE >= OFF[D - 1]), 0.05))
def check_inputs(d):
    bad = []; v = d["dg"].astype(np.float32); k = d["kids"].astype(np.int64)
    if not (np.isfinite(v).all() and (v == np.floor(v)).all() and v.min() >= 0 and v.max() <= 255): bad.append("symbols")
    if k.min() < 0 or k.max() >= P: return bad + ["children"]
    pl = places(k)
    if (np.sort(pl, axis=-1) != NODE).any(): bad.append("places")
    elif np.take_along_axis(k.reshape(N, 8, 4, P), pl[:, :, None, I:], 3).any(): bad.append("leaves")
    if bad: return bad
    v = logical(d["dg"], pl)
    for m in MEETS:
        o = opened(v, m)
        if max(int(np.count_nonzero(o[..., OFF[t]:OFF[t + 1]], axis=-1).max()) for t in range(D + 1)) > CAP: return ["open nodes"]
        v = meet(v, m)
    return []
def reference(dg, kids):
    pl = places(kids); v = logical(dg, pl)
    for m in MEETS:
        v = meet(v, m)
    y = np.zeros((N, 8, 16, P), np.float32); np.put_along_axis(y, pl[:, :, None], v.astype(np.float32), 3)
    return {"y": y.reshape(N, 128, P).astype(BF)}

from concourse.mybir import AluOpType as A, ActivationFunctionType as F

P, SH, CAP, UP = 2728, 1536.0, 96, 32.0
WD = P + 4 * CAP
SPLIT, LA = True, 640
bf, f32, f16, i32, u16 = "bfloat16", "float32", "float16", "int32", "uint16"


def _sb(n, d):
    return ("sbuf", [128, n], d)


SCRATCH = {
    "DG": _sb(WD, bf), "KW": _sb(P, i32), "RT": _sb(8, bf), "RTO": _sb(8, bf),
    "GB": _sb(8, bf), "X": _sb(144, f32), "X4": _sb(144, f32), "X16": _sb(128, f32), "CF": _sb(24, f32),
    "W": _sb(144, bf), "U": _sb(144, bf), "U4": _sb(144, bf), "BO": _sb(128, bf), "QM": _sb(16, f32),
    "I1": _sb(128, bf), "I3": _sb(128, bf), "I5": _sb(128, bf), "I7": _sb(128, bf), "NI": _sb(128, bf),
    "S15": _sb(128, bf), "NS15": _sb(128, bf), "Y1": _sb(144, bf), "Y2": _sb(144, bf), "SEL": _sb(512, bf),
    "PK": _sb(144, bf), "U2": _sb(144, bf), "U42": _sb(144, bf), "H0": _sb(128, bf), "H1": _sb(128, bf),
    "U8": _sb(136, bf), "U28": _sb(136, bf), "MSK": _sb(192, bf), "RP": _sb(192, bf),
    "T0": _sb(128, f32), "TRI": _sb(128, f32), "JT": _sb(32, f32), "NEG": _sb(32, bf),
    "CB": _sb(512, bf), "JH": _sb(512, bf), "JL": _sb(512, bf),
    "G0": _sb(8, f16), "G1": _sb(32, f16), "G2": _sb(128, f16), "G3": _sb(512, f16), "GX": _sb(512, f32),
    "LI": _sb(48, u16), "L4": _sb(128, u16), "IN": _sb(672, bf), "LV": _sb(2048, bf),
    "PKD": _sb(336, u16), "PKO": _sb(336, u16), "PKF": _sb(336, f32),
    "FL": _sb(672, bf), "F0": _sb(8, bf), "FS": _sb(192, bf), "DS": _sb(32, f32), "ES": _sb(32, f32), "SS": _sb(32, f32),
    "POS": _sb(32, u16), "CA": _sb(704, f32), "CS": _sb(704, f32), "CM": _sb(96, f32), "C16": _sb(96, f16),
    "LB1": _sb(24, u16), "LB2": _sb(24, u16), "LN1": _sb(8, u16), "LN2": _sb(8, u16), "LP": _sb(8, u16), "LNO": _sb(8, u16),
    "MB1": _sb(384, bf), "MB2": _sb(384, bf), "OB1": _sb(384, bf), "OB2": _sb(384, bf),
    "TK": _sb(384, bf), "TD": _sb(384, bf), "QB": _sb(96, bf), "PM1": _sb(96, bf), "PM2": _sb(96, bf), "OP": _sb(96, bf),
    "Q3": _sb(512, bf), "R3": _sb(608, bf), "R3O": _sb(512, bf), "E": _sb(608, bf), "GN": _sb(96, bf),
    "QU": _sb(168, bf), "MU": _sb(168, bf),
}
for _b in range(8):
    SCRATCH["PS%d" % _b] = ("psum", [128, 512], f32)
MSG = ["rt", "a1", "b1", "ln", "r3", "a2", "b2"]
DMAS = ["dga", "dgb", "drt", "dk1", "dk2", "dk3", "dy1", "dy2"]
SEMAPHORES = ["cV", "cS", "cP", "cG"] + ["in_" + m for m in MSG] + ["out_" + m for m in MSG] + DMAS


def _emit(g, T, ops):
    queue = {"V": g.vector, "S": g.scalar, "P": g.tensor, "G": g, "Y": g.sync}
    last_w, readers, bank = {}, {}, {}
    seq = {e: 0 for e in queue}
    known = {e: ({}, set()) for e in queue}
    clock, waits, signal = [], [], set()
    for n, op in enumerate(ops):
        e = op["eng"]
        deps = set(op["after"])
        for r in op["r"]:
            if r in last_w:
                deps.add(last_w[r])
        for w in op["w"]:
            if w in last_w:
                deps.add(last_w[w])
            deps.update(readers.get(w, []))
        for k in op["r"] + op["w"]:
            if k.startswith("PS"):
                deps.update(m for e2, m in bank.get(k[:3], {}).items() if e2 != e)
        mine = []
        kv, ks = known[e]
        for d in sorted(deps, reverse=True):
            od = ops[d]
            if od["sem"] is not None:
                if d in ks:
                    continue
                ks.add(d)
            else:
                if od["eng"] == "P" and e == "P":
                    continue
                if kv.get(od["eng"], 0) >= od["seq"]:
                    continue
                kv[od["eng"]] = od["seq"]
                signal.add(d)
            mine.append(d)
            for e2, s in clock[d][0].items():
                kv[e2] = max(kv.get(e2, 0), s)
            ks.update(clock[d][1])
        seq[e] += 1
        op["seq"] = seq[e]
        arrival = op["fn"] is None and op["sem"] is not None
        clock.append(({}, set()) if arrival else (dict(kv), set(ks)))
        waits.append(mine)
        for r in op["r"]:
            readers.setdefault(r, []).append(n)
        for w in op["w"]:
            last_w[w] = n
            readers[w] = []
        for k in op["r"] + op["w"]:
            if k.startswith("PS"):
                bank.setdefault(k[:3], {})[e] = n
    count = {e: 0 for e in queue}
    for n, op in enumerate(ops):
        e = op["eng"]
        for d in waits[n]:
            od = ops[d]
            if od["sem"] is not None:
                queue[e].wait_ge(T.sem[od["sem"]], od["n"])
            else:
                queue[e].wait_ge(T.sem["c" + od["eng"]], od["count"])
        if op["fn"] is None:
            continue
        ins = op["fn"]()
        if op["sem"] is None and n in signal:
            count[e] += 1
            op["count"] = count[e]
            ins.then_inc(T.sem["c" + e], 1)


def rank_program(g, core, T, topo):
    rank = T.rank_of(core)
    if rank is None:
        return
    p1, p2 = T.cores[rank ^ 1], T.cores[rank ^ 2]
    ops = []
    v, s, pe = g.vector, g.scalar, g.tensor

    def add(eng, fn, r, w, sem=None, n=0, after=()):
        ops.append({"eng": eng, "fn": fn, "r": list(r), "w": list(w), "sem": sem, "n": n, "after": list(after)})
        return len(ops) - 1

    def ts(out, in0, a, op0, r, w, b=None, op1=None):
        if op1 is None:
            return add("V", lambda: v.tensor_scalar(out, in0, a, None, op0), r, w)
        return add("V", lambda: v.tensor_scalar(out, in0, a, b, op0, op1), r, w)

    def tt(out, in0, in1, op, r, w):
        return add("V", lambda: v.tensor_tensor(out, in0, in1, op), r, w)

    def cp(out, in_, r, w):
        return add("V", lambda: v.tensor_copy(out, in_), r, w)

    def ms(ap, c, w, r=()):
        return add("V", lambda: v.memset(ap, c), r, w)

    def scan(out, d0, d1, init, op0, op1, r, w):
        return add("V", lambda: v.tensor_tensor_scan(out, d0, d1, init, op0, op1), r, w)

    def act(out, in_, r, w, func=F.Identity, **kw):
        return add("S", lambda: s.activation(out, in_, func, **kw), r, w)

    def mm(out, lhsT, rhs, start, stop, r, w):
        return add("P", lambda: pe.matmul(out, lhsT, rhs, start, stop), r, w)

    def iota(out, pat, cm, w, fl=True):
        if fl:
            return add("G", lambda: g.iota(out, pat, 0, cm, allow_small_or_imprecise_dtypes=True), [], w)
        return add("G", lambda: g.iota(out, pat, 0, cm), [], w)

    def dma(eng, out, in_, sem, r, w):
        q = g.sync if eng == "Y" else g.scalar
        return add(eng, lambda: q.dma_start(out, in_).then_inc(T.sem[sem], 16), r, w, sem=sem, n=16)

    sent = []

    def send(name, dst, out, in_, r, land):
        rid, pid = topo.addr(dst, core)
        n = len(topo.engines(core, dst))
        m = topo.mask(core, dst)
        sent.append(add("G", lambda: g.remote_dma(out, in_, T.sem["in_" + name], T.sem["out_" + name], pid, rid, m),
                        r, [], sem="out_" + name, n=n))
        add("G", None, [], [land], sem="in_" + name, n=len(topo.engines(dst, core)))

    PS = [T["PS%d" % b] for b in range(8)]
    pc, q_, g16, cw, shc, inic, c1, cj, c2, pre, u_, nu, cu, c4u, cpk, wt = [T.CF[:, j:j + 1] for j in range(16)]
    KW = ["KW1", "KW2", "KW3"]
    DGR = ["DGa", "DGb", "DGx"]
    IW = [T.I1, T.I3, T.I5, T.I7]
    IK = ["I1", "I3", "I5", "I7"]
    dgw, kww = T.DG[:, 0:WD], T.KW[:, 0:P]
    ka, kb, da = 1024, 2048, 1024

    dma("S", T.RT[:], T.dg[:, 0:8], "drt", [], ["RT"])
    dma("Y", T.DG[:, 0:da], T.dg[:, 0:da], "dga", [], ["DGa"])
    iota(pc, [[0, 1]], 1, ["pc"])
    ms(T.KW[:, 0:ka], 0, ["KW1"])
    iota(T.KW[:, kb:P], [[0, P - kb]], 0, ["KW3"], fl=False)
    dma("Y", T.KW[0:128:4, 0:ka], T.kids[:, 0:ka], "dk1", [], ["KW1"])
    ms(T.KW[:, ka:kb], 0, ["KW2"])
    dma("Y", T.KW[0:128:4, kb:P], T.kids[:, kb:P], "dk3", [], ["KW3"])
    dma("Y", T.KW[0:128:4, ka:kb], T.kids[:, ka:kb], "dk2", [], ["KW2"])
    dma("Y", T.DG[:, da:P], T.dg[:, da:P], "dgb", [], ["DGb"])
    iota(T.X[:], [[1, 144]], 0, ["X"])
    iota(T.X16[:], [[16, 8], [0, 16]], 0, ["X16"])
    send("rt", p1, T.RTO[:], T.RT[:], ["RT"], "RTO")
    iota(T.X4[:], [[4, 36], [0, 4]], 0, ["X4"])
    iota(T.JH[:], [[16, 32], [0, 16]], 0, ["JH"])
    iota(T.JL[:], [[0, 32], [1, 16]], 0, ["JL"])

    act(T.GB[:, 0:1], pc, ["pc"], ["GB0"], bias=3072 - 7.5)
    act(T.GB[:, 1:2], pc, ["pc"], ["GB1"], bias=1536 - 3.5)
    act(g16, T.GB[:, 0:1], ["GB0"], ["g16"], bias=-3072.0)
    act(q_, g16, ["g16", "pc"], ["q"], scale=-1.0, bias=pc)
    act(cw, q_, ["q", "g16"], ["cw"], scale=0.25, bias=g16)
    act(c1, q_, ["q"], ["c1"], scale=16.0, bias=144.0)
    act(inic, q_, ["q"], ["inic"], scale=-32.0, bias=-96.0)
    act(c2, q_, ["q"], ["c2"], scale=24.0, bias=P + UP)
    act(cj, c1, ["c1", "q"], ["cj"], scale=q_, bias=96.0)
    act(nu, T.GB[:, 1:2], ["GB1"], ["nu"], bias=-1536.0)
    act(c4u, g16, ["g16", "nu"], ["c4u"], scale=-1.0, bias=nu)
    act(u_, c4u, ["c4u"], ["u"], scale=0.125)
    act(wt, u_, ["u"], ["wt"], scale=255.0, bias=1.0)
    act(cu, u_, ["u", "g16"], ["cu"], bias=g16)
    act(nu, u_, ["u"], ["nu"], scale=-1.0, bias=1.0)
    act(c4u, u_, ["u", "g16"], ["c4u"], scale=4.0, bias=g16)
    act(cpk, nu, ["nu", "pc"], ["cpk"], scale=8.0, bias=pc)
    ts(T.W[:], T.X[:], 12.0, A.subtract, ["X", "cw"], ["W"], cw, A.is_equal)
    ts(T.QM[:], T.X[:, 0:16], q_, A.is_equal, ["X", "q"], ["QM"])
    ts(T.U[:], T.X[:], 15.0, A.subtract, ["X", "g16"], ["U"], g16, A.is_equal)
    ts(T.I1[:], T.X[:, 0:128], pc, A.is_equal, ["X", "pc"], ["I1"])
    ts(T.BO[:], T.X16[:], g16, A.is_equal, ["X16", "g16"], ["BO"])
    ms(T.RP[:], 0.0, ["RP"])
    ms(T.MSK[:], 0.0, ["MSK"])
    ms(T.DG[:, P:WD], 0.0, ["DGx"])
    act(pre, T.QM[:, 1:2], ["QM", "c2"], ["pre"], scale=512 - P - 24.0, bias=c2)
    act(shc, T.QM[:, 2:3], ["QM"], ["shc"], scale=-SH, bias=SH)

    def prefill():
        act(T.CA[:, 0:CAP], T.X[:, 0:CAP], ["X", "pre"], ["CA"], func=F.Silu if SPLIT else F.Identity, bias=pre)
        if SPLIT:
            act(T.CS[:, 0:CAP], T.X[:, 0:CAP], ["X", "pre"], ["CS"], func=F.Silu, bias=pre)

    prefill()
    act(T.Y1[:], T.U[:], ["U", "QM"], ["Y1"], scale=T.QM[:, 1:2])
    for k in range(4):
        act(T.SEL[:, 128 * k:128 * k + 128], T.U[:, 13:141], ["U", "QM"], ["SEL%d" % k], scale=T.QM[:, 4 * k:4 * k + 1])
    act(T.T0[:], T.BO[:], ["BO"], ["T0"])
    act(T.JT[:], T.X[:, 0:32], ["X", "cj"], ["JT"], bias=cj)

    def wrap4(ps, src, rk, pk):
        for m in range(4):
            mm(ps, T.W[:, 12 - 4 * m:140 - 4 * m], src[:, m::4], m == 0, m == 3, ["W", rk], [pk])

    def wrap16(ps, mat, mk, src, rk, pk):
        for q in range(16):
            mm(ps, mat[:, 15 - q:143 - q], src[:, q::16], q == 0, q == 15, [mk, rk], [pk])

    ts(T.G0[:], T.KW[:, 0:8], SH, A.subtract, ["KW1"], ["G0"])
    wrap4(PS[0][:, 0:2], T.G0, "G0", "PS0")
    ts(T.PK[:], T.X[:], cpk, A.is_equal, ["X", "cpk", "wt"], ["PK"], wt, A.mult)
    ts(T.LI[:, 0:2], PS[0][:, 0:2], SH, A.add, ["PS0"], ["L1"])
    ms(T.RP[:, 0::6], 1.0, ["RP"])
    ms(T.MSK[:, 5::6], 1.0, ["MSKc"], ["MSK"])
    ts(T.G1[:], kww.indirect(T.LI[:, 0:2]), SH, A.subtract, KW + ["L1"], ["G1"])
    wrap4(PS[0][:, 2:10], T.G1, "G1", "PS0")
    ts(T.U2[:], T.X[:], 14.0, A.subtract, ["X", "cu"], ["U2"], cu, A.is_equal)
    ts(T.LI[:, 2:10], PS[0][:, 2:10], SH, A.add, ["PS0"], ["L2"])
    ts(T.G2[:], kww.indirect(T.LI[:, 2:10]), SH, A.subtract, KW + ["L2"], ["G2"])
    wrap4(PS[0][:, 10:42], T.G2, "G2", "PS0")
    mm(PS[7][:], T.Y1[:, 14:142], T.JH[:], True, False, ["Y1", "JH"], ["PS7"])
    ts(T.U42[:], T.X4[:], 8.0, A.subtract, ["X4", "c4u"], ["U42"], c4u, A.is_equal)
    ts(T.LI[:, 10:42], PS[0][:, 10:42], SH, A.add, ["PS0"], ["L3"])
    ms(T.CB[:], 3072.0, ["CB"])
    cp(T.IN[:, 0:352], dgw.indirect(T.LI[:, 0:22]), DGR + ["L1", "L2", "L3"], ["INa"])
    act(T.IN[:, 352:672], dgw.indirect(T.LI[:, 22:42]), DGR + ["L3"], ["INb"], func=F.Copy)
    for u in range(2):
        mm(PS[4][:, 0:176], T.PK[:, 8 - 8 * u:136 - 8 * u], T.IN[:, u:352:2], u == 0, u == 1, ["PK", "INa"], ["PS4"])
    for u in range(2):
        mm(PS[5][:, 0:160], T.PK[:, 8 - 8 * u:136 - 8 * u], T.IN[:, 352 + u:672:2], u == 0, u == 1, ["PK", "INb"], ["PS5"])
    cp(T.PKD[:, 0:176], PS[4][:, 0:176], ["PS4"], ["PKDa"])
    cp(T.PKD[:, 176:336], PS[5][:, 0:160], ["PS5"], ["PKDb"])
    send("a1", p1, T.PKO[:], T.PKD[:], ["PKDa", "PKDb"], "PKO")
    add("G", lambda: g.affine_select(T.TRI[:], T.T0[:], [[1, 128]], A.is_gt, 0.0, 0, -1), ["T0"], ["TRI"])

    mm(PS[7][:], T.Y1[:, 14:142], T.JL[:], False, False, ["Y1", "JL"], ["PS7"])
    for k in range(4):
        mm(PS[7][:, k::4], T.SEL[:, 128 * k:128 * k + 128], T.G2[:], False, False, ["SEL%d" % k, "G2"], ["PS7"])
    ts(T.G3[:], kww.indirect(T.LI[:, 10:42]), shc, A.subtract, KW + ["L3", "shc"], ["G3"])
    act(T.MSK[:, 0::6], T.X[:, 0:32], ["X", "u", "MSK"], ["MSKa"], scale=0.0, bias=u_)
    act(T.MSK[:, 3::6], T.X[:, 0:32], ["X", "nu", "MSK"], ["MSKb"], scale=0.0, bias=nu)
    act(T.H0[:], T.BO[:], ["BO", "nu"], ["H0"], scale=nu)
    act(T.H1[:], T.BO[:], ["BO", "u"], ["H1"], scale=u_)
    for k in range(1, 4):
        act(IW[k][:], T.I1[:], ["I1"], [IK[k]], scale=float(2 * k + 1))
    act(T.S15[:], T.BO[:], ["BO", "QM"], ["S15"], scale=T.QM[:, 15:16])
    act(T.NI[:], T.I1[:], ["I1"], ["NI"], scale=-1.0)
    act(T.Y2[:], T.U[:], ["U", "QM"], ["Y2"], scale=T.QM[:, 2:3])
    act(T.NS15[:], T.S15[:], ["S15"], ["NS15"], scale=-1.0)
    wrap4(PS[0][:, 64:192], T.G3, "G3", "PS0")
    tt(T.U28[:], T.U2[:, 0:136], T.U2[:, 8:144], A.add, ["U2"], ["U28"])
    ts(T.L4[:], PS[0][:, 64:192], SH, A.add, ["PS0"], ["L4"])
    mm(PS[7][:], T.I1[:], T.G3[:], False, True, ["I1", "G3"], ["PS7"])
    act(T.LV[:, LA:2048], dgw.indirect(T.L4[:, LA // 16:128]), DGR + ["L4"], ["LVb"], func=F.Copy)
    act(T.GX[:], PS[7][:], ["PS7"], ["GX"], bias=SH + UP)
    cp(T.LV[:, 0:LA], dgw.indirect(T.L4[:, 0:LA // 16]), DGR + ["L4"], ["LVa"])
    tt(T.F0[:], T.RT[:], T.RTO[:], A.not_equal, ["RT", "RTO"], ["F0"])
    ms(T.NEG[:], -1.0, ["NEG"])

    X = PS[3]

    def count_start():
        mm(X[:, 0:192], T.I1[:], T.MSK[:], True, False, ["I1", "MSK", "MSKa", "MSKb", "MSKc"], ["PS3"])

    def count0(src, rk, stop):
        for e in range(4):
            mm(X[:, 6 * e + 1:192:24], T.BO[:], src, False, stop and e == 3, ["BO", rk], ["PS3"])

    def count3(rs):
        for r in rs:
            mm(X[:, 0:192:3], T.U8[:, 7 - r:135 - r], T.FL[:, 160 + r:672:8], False, False, ["U8", "FLa", "FLb"], ["PS3"])

    def compact(LB, lbk, MB, mbk, between):
        f = T.FS[:, 5::6]
        scan(T.FS[:], T.RP[:], X[:, 0:192], 0.0, A.max, A.min, ["RP", "PS3"], ["FS"])
        scan(T.DS[:], T.NEG[:], f, inic, A.add, A.add, ["NEG", "FS", "inic"], ["DS"])
        mm(PS[0][:, 256:257], T.TRI[:], T.DS[:, 31:32], True, True, ["TRI", "DS"], ["PS0"])
        between()
        tt(T.ES[:], T.DS[:], f, A.mult, ["DS", "FS"], ["ES"])
        tt(T.SS[:], T.ES[:], T.JT[:], A.add, ["ES", "JT"], ["SS"])
        ts(T.POS[:], T.SS[:], PS[0][:, 256:257], A.add, ["SS", "PS0"], ["POS"])
        if SPLIT:
            cp(T.CA[:, 0:704].indirect(T.POS[:, 0:16]), T.GX[:, 0:256], ["GX", "POS"], ["CA"])
            act(T.CS[:, 0:704].indirect(T.POS[:, 16:32]), T.GX[:, 256:512], ["GX", "POS"], ["CS"], func=F.Silu)
            tt(T.CM[:], T.CA[:, 0:CAP], T.CS[:, 0:CAP], A.min, ["CA", "CS"], ["CM"])
            ts(T.C16[:], T.CM[:], SH + UP, A.subtract, ["CM"], ["C16"])
        else:
            cp(T.CA[:, 0:704].indirect(T.POS[:]), T.GX[:], ["GX", "POS"], ["CA"])
            ts(T.C16[:], T.CA[:, 0:CAP], SH + UP, A.subtract, ["CA"], ["C16"])
        wrap4(PS[0][:, 200:224], T.C16, "C16", "PS0")
        ts(LB[:], PS[0][:, 200:224], SH + 0.25, A.add, ["PS0"], [lbk])
        cp(MB[:, 0:192], dgw.indirect(LB[:, 0:12]), DGR + [lbk], [mbk + "a"])
        act(MB[:, 192:384], dgw.indirect(LB[:, 12:24]), DGR + [lbk], [mbk + "b"], func=F.Copy)

    def bias(ps, n, pk):
        mm(ps, T.BO[:], T.CB[:, 0:n], True, False, ["BO", "CB"], [pk])

    def weigh(ps, buf, a, n, rk, pk, stop):
        for k in range(4):
            mm(ps, IW[k][:], buf[:, a + k:a + 4 * n:4], False, stop and k == 3, [IK[k]] + rk, [pk])

    def before_leaves(MB, mbk):
        mk = [mbk + "a", mbk + "b"]
        mm(PS[4][:, 0:384], T.NS15[:], MB[:], True, False, ["NS15"] + mk, ["PS4"])
        mm(PS[5][:, 0:384], T.NI[:], MB[:], True, False, ["NI"] + mk, ["PS5"])
        bias(PS[6][:, 0:CAP], CAP, "PS6")
        weigh(PS[6][:, 0:CAP], MB, 0, CAP, mk, "PS6", False)

    def after_leaves(OB, obk):
        mm(PS[4][:, 0:384], T.S15[:], OB[:], False, True, ["S15", obk], ["PS4"])
        mm(PS[5][:, 0:384], T.I1[:], OB[:], False, True, ["I1", obk], ["PS5"])
        ts(T.TK[:], PS[4][:, 0:384], 0.0, A.is_gt, ["PS4"], ["TK"])
        tt(T.TD[:], T.TK[:], PS[5][:, 0:384], A.mult, ["TK", "PS5"], ["TD"])
        weigh(PS[6][:, 0:CAP], T.TD, 0, CAP, ["TD"], "PS6", True)

    def rebuild3(a, b, rk):
        bias(PS[1][:, a // 4:b // 4], (b - a) // 4, "PS1")
        weigh(PS[1][:, a // 4:b // 4], T.LV, a, (b - a) // 4, [rk], "PS1", True)

    count_start()
    rebuild3(0, LA, "LVa")
    count0(T.F0[:], "F0", False)
    cp(T.PKF[:], T.PKO[:], ["PKO"], ["PKF"])
    tt(T.FL[:, 0:176], T.PKF[:, 0:176], PS[4][:, 0:176], A.not_equal, ["PKF", "PS4"], ["FLa"])
    tt(T.FL[:, 176:336], T.PKF[:, 176:336], PS[5][:, 0:160], A.not_equal, ["PKF", "PS5"], ["FLb"])
    for u in range(2):
        mm(X[:, 6 * u + 2:192:12], T["H%d" % u][:], T.FL[:, 0:16], False, False, ["H%d" % u, "FLa"], ["PS3"])
    for r in range(2):
        mm(X[:, 4:192:6], T.U42[:, 8 - 8 * r:136 - 8 * r], T.FL[:, 16 + r:80:2], False, False, ["U42", "FLa"], ["PS3"])
    for r in range(4):
        mm(X[:, 0:192:3], T.U28[:, 6 - 2 * r:134 - 2 * r], T.FL[:, 80 + r:336:4], False, r == 3, ["U28", "FLa", "FLb"], ["PS3"])
    compact(T.LB1, "LB1", T.MB1, "MB1", lambda: rebuild3(LA, 2048, "LVb"))
    send("b1", p1, T.OB1[:], T.MB1[:], ["MB1a", "MB1b"], "OB1")
    act(T.Q3[:], PS[1][:], ["PS1"], ["Q3"], bias=-127.5)
    wrap16(PS[0][:, 232:238], T.Y1, "Y1", T.C16, "C16", "PS0")
    tt(T.R3[:, 0:512], PS[1][:], T.Q3[:], A.subtract, ["PS1", "Q3"], ["R3"])
    send("r3", p2, T.R3O[:], T.R3[:, 0:512], ["R3"], "R3O")
    ts(T.LN1[:, 0:6], PS[0][:, 232:238], SH + 0.25, A.add, ["PS0"], ["LN1"])
    send("ln", p2, T.LNO[:, 0:6], T.LN1[:, 0:6], ["LN1"], "LNO")
    ms(T.R3[:, 512:608], 0.0, ["R3x"])
    ms(T.E[:, 512:608], 0.0, ["Ex"])
    ts(T.U4[:], T.X4[:], 12.0, A.subtract, ["X4", "g16"], ["U4"], g16, A.is_equal)
    tt(T.U8[:], T.U[:, 0:136], T.U[:, 8:144], A.add, ["U"], ["U8"])
    prefill()
    count_start()
    before_leaves(T.MB1, "MB1")
    after_leaves(T.OB1, "OB1")
    ts(T.QB[:], PS[6][:, 0:CAP], -127.5, A.add, ["PS6"], ["QB"])
    tt(T.PM1[:], PS[6][:, 0:CAP], T.QB[:], A.subtract, ["PS6", "QB"], ["PM1"])
    send("a2", p2, T.OP[:], T.PM1[:], ["PM1"], "OP")

    r3w, ew = T.R3[:, 0:608], T.E[:, 0:608]
    cp(r3w.indirect(T.LN1[:, 0:6]), T.PM1[:], ["PM1", "LN1"], ["R3", "R3x"])
    mm(PS[1][:], T.NI[:], T.R3[:, 0:512], True, False, ["NI", "R3"], ["PS1"])
    mm(PS[1][:], T.I1[:], T.R3O[:], False, True, ["I1", "R3O"], ["PS1"])
    act(T.E[:, 0:512], PS[1][:], ["PS1"], ["E"], func=F.Copy)
    ts(T.GN[:], r3w.indirect(T.LNO[:, 0:6]), -1.0, A.mult, ["R3", "R3x", "LNO"], ["GN"])
    tt(dgw.indirect(T.LB1[:]), T.MB1[:], T.TD[:], A.add, ["MB1a", "MB1b", "TD", "LB1"], DGR)
    bias(PS[7][:, 0:128], 128, "PS7")
    bias(PS[2][:, 0:32], 32, "PS2")
    bias(PS[1][:, 0:8], 8, "PS1")
    tt(ew.indirect(T.LNO[:, 0:6]), T.OP[:], T.GN[:], A.add, ["OP", "GN", "LNO"], ["E", "Ex"])
    weigh(PS[7][:, 0:128], T.E, 0, 128, ["E"], "PS7", True)
    act(T.FL[:, 160:672], T.E[:, 0:512], ["E"], ["FLa", "FLb"], func=F.Abs)

    def modv(ps, pk, a, n, key):
        ts(T.QU[:, a:a + n], ps, -127.5, A.add, [pk], ["Q" + key])
        tt(T.MU[:, a:a + n], ps, T.QU[:, a:a + n], A.subtract, [pk, "Q" + key], ["M" + key])

    modv(PS[7][:, 0:128], "PS7", 32, 128, "u2")
    count3(range(0, 5))
    weigh(PS[2][:, 0:32], T.MU, 32, 32, ["Mu2"], "PS2", True)
    modv(PS[2][:, 0:32], "PS2", 0, 32, "u1")
    count3(range(5, 8))
    weigh(PS[1][:, 0:8], T.MU, 0, 8, ["Mu1"], "PS1", True)
    modv(PS[1][:, 0:8], "PS1", 160, 8, "u0")
    mm(X[:, 2:192:6], T.BO[:], T.MU[:, 0:32], False, False, ["BO", "Mu1"], ["PS3"])
    for m in range(4):
        mm(X[:, 4:192:6], T.U4[:, 12 - 4 * m:140 - 4 * m], T.MU[:, 32 + m:160:4], False, False, ["U4", "Mu2"], ["PS3"])
    count0(T.MU[:, 160:168], "Mu0", True)
    compact(T.LB2, "LB2", T.MB2, "MB2", lambda: None)
    send("b2", p2, T.OB2[:], T.MB2[:], ["MB2a", "MB2b"], "OB2")
    wrap16(PS[0][:, 232:238], T.Y1, "Y1", T.C16, "C16", "PS0")
    wrap16(PS[0][:, 240:246], T.Y2, "Y2", T.C16, "C16", "PS0")
    cp(dgw.indirect(T.LI[:, 10:42]), T.R3[:, 0:512], ["R3", "L3"], DGR)
    ts(T.LN2[:, 0:6], PS[0][:, 232:238], SH + 0.25, A.add, ["PS0"], ["LN2"])
    ts(T.LP[:, 0:6], PS[0][:, 240:246], SH + 0.25, A.add, ["PS0"], ["LP"])
    before_leaves(T.MB2, "MB2")
    bias(PS[7][:, 0:128], 128, "PS7")
    bias(PS[2][:, 0:32], 32, "PS2")
    bias(PS[1][:, 0:8], 8, "PS1")
    after_leaves(T.OB2, "OB2")

    act(T.QB[:], PS[6][:, 0:CAP], ["PS6"], ["QB"], bias=-127.5)
    tt(dgw.indirect(T.LB2[:, 0:12]), T.MB2[:, 0:192], T.TD[:, 0:192], A.add, ["MB2a", "TD", "LB2"], DGR)
    tt(T.PM2[:], PS[6][:, 0:CAP], T.QB[:], A.subtract, ["PS6", "QB"], ["PM2"])
    cp(r3w.indirect(T.LN2[:, 0:6]), T.PM2[:], ["PM2", "LN2"], ["R3", "R3x"])
    weigh(PS[7][:, 0:128], T.R3, 0, 128, ["R3"], "PS7", True)
    act(T.QU[:, 32:160], PS[7][:, 0:128], ["PS7"], ["Qu2"], bias=-127.5)
    tt(dgw.indirect(T.LB2[:, 12:24]), T.MB2[:, 192:384], T.TD[:, 192:384], A.add, ["MB2b", "TD", "LB2"], DGR)
    tt(T.MU[:, 32:160], PS[7][:, 0:128], T.QU[:, 32:160], A.subtract, ["PS7", "Qu2"], ["Mu2"])
    weigh(PS[2][:, 0:32], T.MU, 32, 32, ["Mu2"], "PS2", True)
    act(T.QU[:, 0:32], PS[2][:, 0:32], ["PS2"], ["Qu1"], bias=-127.5)
    cp(dgw.indirect(T.LP[:, 0:6]), T.PM2[:], ["PM2", "LP"], DGR)
    tt(T.MU[:, 0:32], PS[2][:, 0:32], T.QU[:, 0:32], A.subtract, ["PS2", "Qu1"], ["Mu1"])
    weigh(PS[1][:, 0:8], T.MU, 0, 8, ["Mu1"], "PS1", True)
    act(T.QU[:, 160:168], PS[1][:, 0:8], ["PS1"], ["Qu0"], bias=-127.5)
    cp(dgw.indirect(T.LI[:, 0:10]), T.MU[:, 0:160], ["Mu1", "Mu2", "L1", "L2"], DGR)
    tt(T.DG[:, 0:8], PS[1][:, 0:8], T.QU[:, 160:168], A.subtract, ["PS1", "Qu0"], DGR)
    y1 = dma("Y", T.y[0:64, :], T.DG[0:64, 0:P], "dy1", DGR, [])
    y2 = dma("S", T.y[64:128, :], T.DG[64:128, 0:P], "dy2", DGR, [])
    add("G", None, [], [], after=sent)
    add("Y", None, [], [], after=[y1, y2])
    _emit(g, T, ops)
